import numpy as np
import ml_dtypes


def mxq(x, axis, fmt="e4m3"):
    dtype, down = {"e4m3": (ml_dtypes.float8_e4m3fn, 7), "e5m2": (ml_dtypes.float8_e5m2, 14)}[fmt]
    v = np.moveaxis(np.asarray(x, np.float32).astype(ml_dtypes.bfloat16).astype(np.float64), axis, -1)
    blocks = v.reshape(v.shape[:-1] + (-1, 32))
    amax = np.abs(blocks).max(-1, keepdims=True)
    byte = np.maximum(np.where(amax > 0, np.frexp(amax)[1] - 1 + 127, 0) - down, 1)
    scale = np.exp2(byte - 127.0)
    codes = (blocks / scale).astype(np.float32).astype(dtype).astype(np.float64)
    return np.moveaxis((codes * scale).reshape(v.shape), -1, axis)


WIDE = False


def mx_kscale(k):
    if not WIDE:
        return np.ones(k)
    levels = np.array([10, -10, 5, -5, 0])
    if k % 512:
        return np.exp2(np.random.permutation(np.resize(levels, k // 32))).repeat(32)
    a = np.empty((k // 512, 16))
    for p in range(k // 512):
        a[p, :8] = np.random.permutation(np.resize(levels, 8))
        for g in range(8):
            far = levels[np.abs(levels - a[p, g]) >= 10]
            a[p, g + 8] = far[np.random.randint(len(far))]
    return np.exp2(a.ravel()).repeat(32)


def f64(x):
    return np.asarray(x).astype(np.float64)


def striped(idx):
    return np.tile(np.asarray(idx).reshape(-1, 16).T, (8, 1)).astype(np.uint16)


def unstriped(offs):
    return offs[:16].T.reshape(-1).astype(np.int64)


E2M1 = np.array([0.0, 0.5, 1.0, 1.5, 2.0, 3.0, 4.0, 6.0, -0.0, -0.5, -1.0, -1.5, -2.0, -3.0, -4.0, -6.0])


def pack_weight(w, fmt):
    k, n = w.shape
    w = f64(np.asarray(w, np.float32).astype(ml_dtypes.bfloat16)).reshape(k // 32, 32, n)
    amax = np.abs(w).max(1)
    if fmt == "e4m3":
        byte = np.frexp(amax)[1] - 1 + 127 - 7
    else:
        mant, ex = np.frexp(amax / 6.0)
        byte = np.where(mant > 0.5, ex, ex - 1) + 127
    byte = np.clip(np.where(amax > 0, byte, 1), 1, 254)
    scaled = (w * np.exp2(127.0 - byte)[:, None, :]).reshape(k, n).astype(np.float32)
    by_word = np.ascontiguousarray(scaled.reshape(k // 512, 128, 4, n).transpose(0, 1, 3, 2))
    if fmt == "e4m3":
        words = by_word.astype(ml_dtypes.float8_e4m3fn).view(np.uint8)
    else:
        c = by_word.astype(ml_dtypes.float4_e2m1fn).view(np.uint8) & 0xF
        words = (c[..., 0::2] | (c[..., 1::2] << 4)).reshape(k // 512, 128, 2 * n)
    return np.ascontiguousarray(words), np.ascontiguousarray(byte.astype(np.uint8).reshape(k // 512, 16, n))


def unpack_weight(words, scales, fmt):
    g, _, n = scales.shape
    words = np.ascontiguousarray(words).reshape(g, 128, n, -1)
    if fmt == "e4m3":
        vals = words.view(ml_dtypes.float8_e4m3fn).astype(np.float64)
    else:
        nib = np.empty((g, 128, n, 4), np.uint8)
        nib[..., 0::2] = words & 0xF
        nib[..., 1::2] = words >> 4
        vals = E2M1[nib]
    vals = vals * np.repeat(np.exp2(scales.astype(np.float64) - 127.0), 8, axis=1)[..., None]
    return vals.transpose(0, 1, 3, 2).reshape(g * 512, n)


D, E, T, I, Q, G, U = 512, 512, 2048, 256, 512, 16, 1024


def setup_inputs():
    n = np.random.standard_normal
    idx = np.random.permutation(T)[:I]
    idx4 = np.random.permutation(U)[:I]
    fd = mx_kscale(D)
    fe = mx_kscale(E)
    fq = mx_kscale(Q)
    keysp = pack_weight(n((D, T)) / fd[:, None], "e2m1")
    valsp = pack_weight(n((E, T)) / fe[:, None], "e2m1")
    return {
        "query": (n((D, Q)) * 0.6 / np.sqrt(D) * fd[:, None]).astype(np.float32),
        "keys_words": keysp[0],
        "keys_scales": keysp[1],
        "trust": (np.random.uniform(0.3, 1.0, (Q, 1))).astype(np.float32),
        "gout": (n((E, Q)) * 1 / np.sqrt(E) * fe[:, None]).astype(np.float32),
        "vals_words": valsp[0],
        "vals_scales": valsp[1],
        "size": (np.random.uniform(0.5, 2.0, (1, I))).astype(np.float32),
        "qs": (np.random.uniform(100.0, 400.0, (Q, 1)) * fq[:, None]).astype(np.float32),
        "qrows": (n((Q, D)) / fq[:, None]).astype(np.float32),
        "old": (n((D, U)) * 4.0).astype(np.float32),
        "fade": (np.random.uniform(0.5, 1.0, (1, U))).astype(np.float32),
        "offs": striped(idx),
        "offs4": striped(idx4),
    }


def reference(query, keys_words, keys_scales, trust, gout, vals_words, vals_scales, size, qs, qrows, old, fade, offs, offs4):
    idx = unstriped(offs)
    idx4 = unstriped(offs4)
    keysu = unpack_weight(keys_words, keys_scales, "e2m1")
    valsu = unpack_weight(vals_words, vals_scales, "e2m1")
    queryq = mxq(f64(query), 0, "e4m3")
    keysidxg = keysu[:, idx]
    a = queryq.T @ keysidxg
    s = a.reshape(Q, G, I // G).mean(axis=2) * f64(trust)
    sr = np.repeat(s, I // G, axis=1)
    b = a - sr
    p = np.exp(b - np.max(b, axis=1, keepdims=True))
    z = np.sum(p, axis=1, keepdims=True)
    goutq = mxq(f64(gout), 0, "e4m3")
    valsidxg = valsu[:, idx]
    c0 = goutq.T @ valsidxg
    dz = np.sum(c0 * p * f64(size) / np.square(z) * (-1.0), axis=1, keepdims=True)
    dp = c0 / z * f64(size) + dz
    db = dp * p
    dsr = db * (-1.0)
    ds = dsr.reshape(Q, G, I // G).sum(axis=2)
    e1 = ds * f64(trust) / 16.0
    r1 = np.repeat(e1, I // G, axis=1)
    da = db + r1
    gs = da * f64(qs)
    qrowsq = mxq(f64(qrows), 0, "e4m3")
    gsq = mxq(gs, 0, "e4m3")
    gk = qrowsq.T @ gsq
    gf = np.zeros((D, U))
    gf[:, idx4] = gk
    y = f64(old) * f64(fade) + gf
    return y

@@ -1,0 +1,343 @@
+from contextlib import ExitStack
+
+import concourse.mybir as mybir
+from concourse.masks import make_identity
+
+D, E, T, I, Q, G, U = 512, 512, 2048, 256, 512, 16, 1024
+FLOPS = 2 * Q * I * (D + E + D)
+
+F32 = mybir.dt.float32
+BF16 = mybir.dt.bfloat16
+I32 = mybir.dt.int32
+U32 = mybir.dt.uint32
+U16 = mybir.dt.uint16
+U8 = mybir.dt.uint8
+FP8X4 = mybir.dt.float8_e4m3fn_x4
+FP4X4 = mybir.dt.float4_e2m1fn_x4
+ALU = mybir.AluOpType
+ACT = mybir.ActivationFunctionType
+AXIS_X = mybir.AxisListType.X
+
+P = 128
+PACK = 4
+PAGE = I // G
+BANK = 512
+HALVES = 2
+
+
+def tile_attend_bpagecentred_k_kernel(
+    tc, query, keys_words, keys_scales, trust, gout, vals_words, vals_scales, size, qs, qrows, old, fade, offs, offs4, out
+):
+    nc = tc.nc
+    with ExitStack() as ctx:
+        sb = ctx.enter_context(tc.tile_pool(name="sb", bufs=1))
+        psum = ctx.enter_context(tc.psum_pool(name="psum", bufs=1))
+
+        def bank_tile(number, name):
+            return psum.tile([P, BANK], F32, name=name, tag=f"bank{number}")
+
+        def tile(shape, dtype, name, tag=None):
+            return sb.tile(shape, dtype, name=name, tag=tag or name, align_bytes=64)
+
+        def load_scale_rows(scales, name):
+            plane = tile([P, T], U8, name)
+            nc.vector.memset(plane[:].bitcast(I32), 0)
+            for quad in range(4):
+                nc.scalar.dma_start(
+                    out=plane[32 * quad : 32 * quad + 4, :].bitcast(I32),
+                    in_=scales[0, 4 * quad : 4 * quad + 4, :].bitcast(I32),
+                )
+            return plane
+
+        def load_words(words, name, tag):
+            pool_words = tile([P, T], U16, name, tag=tag)
+            nc.sync.dma_start(out=pool_words[:].bitcast(I32), in_=words[0].bitcast(I32))
+            return pool_words
+
+        def load_column_halves(matrix, name):
+            halves = []
+            for h in range(HALVES):
+                raw = tile([P, PACK, Q // HALVES], F32, f"{name}{h}")
+                cols = slice(h * Q // HALVES, (h + 1) * Q // HALVES)
+                nc.sync.dma_start(out=raw[:], in_=matrix[:, cols].rearrange("(p j) c -> p j c", j=PACK))
+                halves.append(raw)
+            return halves
+
+        slots = sb.tile([P, I // 16], U16, name="slots")
+        nc.sync.dma_start(slots[:], offs)
+        places = sb.tile([P, I // 16], U16, name="places")
+        nc.sync.dma_start(places[:], offs4)
+        trust_sb = tile([P, PACK], F32, "trust_sb")
+        nc.scalar.dma_start(out=trust_sb[:], in_=trust.rearrange("(p r) o -> p (r o)", r=PACK))
+        qs_sb = tile([P, PACK], F32, "qs_sb")
+        nc.scalar.dma_start(out=qs_sb[:], in_=qs.rearrange("(p r) o -> p (r o)", r=PACK))
+        query_raw = load_column_halves(query, "query_raw")
+        key_plane = load_scale_rows(keys_scales, "key_plane")
+        key_pool = load_words(keys_words, "key_pool", "key_pool")
+        gout_raw = load_column_halves(gout, "gout_raw")
+        rows = tile([P, P], F32, "rows")
+        nc.gpsimd.memset(rows[:], 0.0)
+        nc.scalar.dma_start(out=rows[8:10, :], in_=size.rearrange("o (c p) -> (o c) p", p=P))
+        nc.scalar.dma_start(out=rows[0:8, :], in_=fade.rearrange("o (c p) -> (o c) p", p=P))
+        val_plane = load_scale_rows(vals_scales, "val_plane")
+        ident = tile([P, P], F32, "ident")
+        make_identity(nc, ident[:])
+
+        warm = tile([P, 1], F32, "warm")
+        nc.scalar.activation(out=warm[:], in_=ident[:, 0:1], func=ACT.Exp)
+
+        scattered = []
+        for j in range(2):
+            window = tile([P, U], F32, f"scattered{j}")
+            nc.vector.memset(window[:], 0.0)
+            scattered.append(window)
+
+        def gather(pool_tile, dtype, name):
+            picked = tile([P, I], dtype, name)
+            nc.vector.tensor_copy(out=picked[:], in_=pool_tile[:].indirect(slots[:]))
+            return picked
+
+        def deal_and_round(copy, halves, name):
+            grouped = tile([P, PACK, P, PACK], BF16, name)
+            for h, raw in enumerate(halves):
+                s = slice(h * P // HALVES, (h + 1) * P // HALVES)
+                copy(
+                    out=grouped[:, :, s, :].rearrange("p r s j -> p s j r"),
+                    in_=raw[:].rearrange("p j (s r) -> p s j r", r=PACK),
+                )
+            return grouped[:].rearrange("p r s j -> p (r s j)")
+
+        def quantize(values, name):
+            width = values.shape[1] // PACK
+            codes = tile([P, width], U32, name + "_codes")
+            scales = tile([P, width], U8, name + "_scales")
+            nc.vector.quantize_mx(out=codes[:].bitcast(FP8X4), scales=scales[:], in_=values)
+            return codes, scales
+
+        def product(out_cols, lhs, lhs_dtype, lhs_cols, rhs, rhs_dtype):
+            nc.tensor.matmul_mx(
+                out=out_cols,
+                lhsT=lhs[0][:, lhs_cols].bitcast(lhs_dtype),
+                lhsT_scale=lhs[1][:, lhs_cols],
+                rhs=rhs[0][:].bitcast(rhs_dtype),
+                rhs_scale=rhs[1][:],
+                start=True,
+                stop=True,
+            )
+
+        def rows_times_listed(row_operand, listed, first_bank, name):
+            banks = []
+            for h in range(HALVES):
+                bank = bank_tile(first_bank + h, f"{name}{h}")
+                for rr in range(2):
+                    r = 2 * h + rr
+                    product(bank[:, rr * I : (rr + 1) * I], row_operand, FP8X4, slice(r * P, (r + 1) * P), listed, FP4X4)
+                banks.append(bank)
+            return banks
+
+        def block(n):
+            return slice(n * P, (n + 1) * P)
+
+        query_bf = deal_and_round(nc.vector.tensor_copy, query_raw, "query_bf")
+        val_pool = load_words(vals_words, "val_pool", "query_raw0")
+        key_scales = gather(key_plane, U8, "key_scales")
+        query_mx = quantize(query_bf, "query")
+        key_words = gather(key_pool, U16, "key_words")
+        scores = rows_times_listed(query_mx, (key_words, key_scales), 0, "scores")
+
+        neg_trust = tile([P, PACK], F32, "neg_trust")
+        nc.vector.tensor_scalar(neg_trust[:], trust_sb[:], -1.0 / PAGE, None, ALU.mult)
+
+        turned = bank_tile(4, "turned")
+        nc.tensor.transpose(turned[:, 0:P], rows[:], ident[:])
+        columns = tile([P, 16], F32, "columns")
+        nc.scalar.copy(out=columns[:], in_=turned[:, 0:16])
+        spread = bank_tile(5, "spread")
+        for c in range(I // P):
+            nc.tensor.transpose(spread[:, block(c)], columns[:, 8 + c : 9 + c].to_broadcast([P, P]), ident[:])
+        size_row = tile([P, I], F32, "size_row")
+        nc.scalar.copy(out=size_row[:], in_=spread[:, 0:I])
+
+        gout_bf = deal_and_round(nc.scalar.copy, gout_raw, "gout_bf")
+
+        def load_old(h, tag):
+            part = tile([P, D // P, BANK], F32, f"old{h}", tag=tag)
+            nc.sync.dma_start(out=part[:], in_=old[:, h * BANK : (h + 1) * BANK].rearrange("(j p) u -> p j u", p=P))
+            return part
+
+        old_sb = [load_old(0, "query_raw1")]
+        qrows_raw = tile([P, PACK, D], F32, "qrows_raw", tag="gout_raw0")
+        nc.sync.dma_start(out=qrows_raw[:], in_=qrows.rearrange("(p t) d -> p t d", t=PACK))
+        old_sb.append(load_old(1, "gout_raw1"))
+
+        val_scales = gather(val_plane, U8, "val_scales")
+        val_words = gather(val_pool, U16, "val_words")
+        gout_mx = quantize(gout_bf, "gout")
+        value_scores = rows_times_listed(gout_mx, (val_words, val_scales), 2, "value_scores")
+
+        centred, weights, sums = [], [], []
+        for h in range(HALVES):
+            page_sum = tile([P, 2 * G], F32, f"page_sum{h}")
+            nc.vector.tensor_reduce(
+                out=page_sum[:], in_=scores[h][:].rearrange("p (g j) -> p g j", j=PAGE), axis=AXIS_X, op=ALU.add
+            )
+            b = tile([P, 2, I], F32, f"centred{h}")
+            for rr in range(2):
+                r = 2 * h + rr
+                nc.vector.scalar_tensor_tensor(
+                    out=b[:, rr, :].rearrange("p (g j) -> p g j", j=PAGE),
+                    in0=page_sum[:, rr * G : (rr + 1) * G].unsqueeze(2).to_broadcast([P, G, PAGE]),
+                    scalar=neg_trust[:, r : r + 1],
+                    in1=scores[h][:, rr * I : (rr + 1) * I].rearrange("p (g j) -> p g j", j=PAGE),
+                    op0=ALU.mult,
+                    op1=ALU.add,
+                )
+            centred.append(b)
+        for h in range(HALVES):
+            m = tile([P, 2], F32, f"neg_max{h}")
+            nc.vector.tensor_reduce(out=m[:], in_=centred[h][:], axis=AXIS_X, op=ALU.max, negate=True)
+            p = tile([P, 2, I], F32, f"weights{h}")
+            z = tile([P, 2], F32, f"sums{h}")
+            for rr in range(2):
+                nc.scalar.activation(
+                    out=p[:, rr, :], in_=centred[h][:, rr, :], func=ACT.Exp, bias=m[:, rr : rr + 1], accum_out=z[:, rr : rr + 1]
+                )
+            weights.append(p)
+            sums.append(z)
+
+        qrows_bf = tile([P, D, PACK], BF16, "qrows_bf")
+        for j in range(D // P):
+            nc.scalar.copy(
+                out=qrows_bf[:, block(j), :].rearrange("p (c i) t -> p c t i", i=4),
+                in_=qrows_raw[:, :, block(j)].rearrange("p t (c i) -> p c t i", i=4),
+            )
+
+        db = tile([P, PACK, I], F32, "db")
+        inv, gain, sized, terms, coef = [], [], [], [], []
+        for h in range(HALVES):
+            rz = tile([P, 2], F32, f"inv{h}")
+            nc.vector.reciprocal(out=rz[:], in_=sums[h][:])
+            inv.append(rz)
+            ps = tile([P, 2, I], F32, f"sized{h}")
+            nc.vector.tensor_tensor(ps[:], weights[h][:], size_row[:].unsqueeze(1).to_broadcast([P, 2, I]), ALU.mult)
+            sized.append(ps)
+            k = tile([P, 2], F32, f"gain{h}")
+            nc.vector.tensor_tensor(k[:], inv[h][:], qs_sb[:, 2 * h : 2 * h + 2], ALU.mult)
+            gain.append(k)
+        for h in range(HALVES):
+            w = tile([P, 2, I], F32, f"terms{h}")
+            s = tile([P, 2], F32, f"dots{h}")
+            for rr in range(2):
+                nc.vector.scalar_tensor_tensor(
+                    out=w[:, rr, :],
+                    in0=value_scores[h][:, rr * I : (rr + 1) * I],
+                    scalar=gain[h][:, rr : rr + 1],
+                    in1=sized[h][:, rr, :],
+                    op0=ALU.mult,
+                    op1=ALU.mult,
+                    accum_out=s[:, rr : rr + 1],
+                )
+            c = tile([P, 2], F32, f"coef{h}")
+            nc.vector.scalar_tensor_tensor(out=c[:], in0=s[:], scalar=-1.0, in1=inv[h][:], op0=ALU.mult, op1=ALU.mult)
+            terms.append(w)
+            coef.append(c)
+        for h in range(HALVES):
+            for rr in range(2):
+                nc.vector.scalar_tensor_tensor(
+                    out=db[:, 2 * h + rr, :],
+                    in0=weights[h][:, rr, :],
+                    scalar=coef[h][:, rr : rr + 1],
+                    in1=terms[h][:, rr, :],
+                    op0=ALU.mult,
+                    op1=ALU.add,
+                )
+        qrows_mx = quantize(qrows_bf[:].rearrange("p d t -> p (d t)"), "qrows")
+
+        faded_t = []
+        for c in range(U // P):
+            bank = bank_tile(4 + c % 4, f"old_t{c}")
+            h, cc = divmod(c, BANK // P)
+            for j in range(D // P):
+                nc.tensor.transpose(bank[:, block(j)], old_sb[h][:, j, block(cc)], ident[:])
+            ft = tile([P, D], F32, f"faded_t{c}")
+            nc.scalar.activation(out=ft[:], in_=bank[:], func=ACT.Copy, scale=columns[:, c : c + 1])
+            faded_t.append(ft)
+
+        pages = G // HALVES
+        shifts = []
+        for h in range(HALVES):
+            page_db = tile([P, PACK, pages], F32, f"page_db{h}")
+            nc.vector.tensor_reduce(
+                out=page_db[:], in_=db[:, :, block(h)].rearrange("p r (g j) -> p r g j", j=PAGE), axis=AXIS_X, op=ALU.add
+            )
+            shift = tile([P, pages, PACK], F32, f"shift{h}")
+            nc.vector.tensor_tensor(
+                shift[:].rearrange("p g r -> p r g"),
+                page_db[:],
+                neg_trust[:].unsqueeze(2).to_broadcast([P, PACK, pages]),
+                ALU.mult,
+            )
+            shifts.append(shift)
+        grads = []
+        for h in range(HALVES):
+            gs_bf = tile([P, P, PACK], BF16, f"gs_bf{h}")
+            nc.vector.tensor_tensor(
+                gs_bf[:].rearrange("p (g j) r -> p g j r", j=PAGE),
+                db[:, :, block(h)].rearrange("p r (g j) -> p g j r", j=PAGE),
+                shifts[h][:].unsqueeze(2).to_broadcast([P, pages, PAGE, PACK]),
+                ALU.add,
+            )
+            gs_mx = quantize(gs_bf[:].rearrange("p i r -> p (i r)"), f"gs{h}")
+            bank = bank_tile(h, f"grads{h}")
+            for j in range(D // P):
+                product(bank[:, block(j)], qrows_mx, FP8X4, block(j), gs_mx, FP8X4)
+            gk = tile([P, D // P, P], F32, f"gk{h}")
+            for pair in range(2):
+                nc.scalar.copy(
+                    out=gk[:, 2 * pair : 2 * pair + 2, :].rearrange("p j i -> p (j i)"),
+                    in_=bank[:, 2 * pair * P : (2 * pair + 2) * P],
+                )
+            grads.append(gk)
+
+        first_bank = (2, 4, 0, 6)
+        blocks = BANK // P
+        for j in range(D // P):
+            window = scattered[j % 2]
+            on_tensor = j % 2 == 0
+            faded = []
+            for h in range(HALVES):
+                bank = bank_tile(first_bank[j] + h, f"faded{j}_{h}")
+                for cc in range(blocks):
+                    nc.tensor.matmul(
+                        bank[:, block(cc)],
+                        faded_t[h * blocks + cc][:, block(j)],
+                        ident[:],
+                        start=(cc == 0 or not on_tensor),
+                        stop=not on_tensor,
+                        is_transpose=True,
+                    )
+                faded.append(bank)
+            for h in range(HALVES):
+                nc.vector.tensor_copy(out=window[:].indirect(places[:, 8 * h : 8 * h + 8]), in_=grads[h][:, j, :])
+            for h in range(HALVES):
+                result = tile([P, BANK], F32, f"result{j}_{h}")
+                cols = slice(h * BANK, (h + 1) * BANK)
+                if on_tensor:
+                    bank = bank_tile((6 if j == 0 else 2) + h, f"window_t{j}_{h}")
+                    for cc in range(blocks):
+                        nc.tensor.transpose(bank[:, block(cc)], window[:, block(h * blocks + cc)], ident[:])
+                    window_t = tile([P, BANK], F32, f"window_t{j}_{h}")
+                    nc.scalar.copy(out=window_t[:], in_=bank[:])
+                    for cc in range(blocks):
+                        nc.tensor.matmul(
+                            faded[h][:, block(cc)],
+                            window_t[:, block(cc)],
+                            ident[:],
+                            start=False,
+                            stop=(cc == blocks - 1),
+                            is_transpose=True,
+                        )
+                    nc.scalar.copy(out=result[:], in_=faded[h][:])
+                else:
+                    nc.vector.tensor_tensor(result[:], faded[h][:], window[:, cols], ALU.add)
+                nc.sync.dma_start(out=out[block(j), cols], in_=result[:])

@@ -102,8 +102,8 @@ def tile_attend_bpagecentred_k_kernel(
             for h, raw in enumerate(halves):
                 s = slice(h * P // HALVES, (h + 1) * P // HALVES)
                 copy(
-                    out=grouped[:, :, s, :].rearrange("p r s j -> p s j r"),
-                    in_=raw[:].rearrange("p j (s r) -> p s j r", r=PACK),
+                    out=grouped[:, :, s, :],
+                    in_=raw[:].rearrange("p j (s r) -> p r s j", r=PACK),
                 )
             return grouped[:].rearrange("p r s j -> p (r s j)")
 
@@ -148,6 +148,9 @@ def tile_attend_bpagecentred_k_kernel(
         neg_trust = tile([P, PACK], F32, "neg_trust")
         nc.vector.tensor_scalar(neg_trust[:], trust_sb[:], -1.0 / PAGE, None, ALU.mult)
 
+        neg_qs = tile([P, PACK], F32, "neg_qs")
+        nc.vector.tensor_scalar(neg_qs[:], qs_sb[:], -1.0, None, ALU.mult)
+
         turned = bank_tile(4, "turned")
         nc.tensor.transpose(turned[:, 0:P], rows[:], ident[:])
         columns = tile([P, 16], F32, "columns")
@@ -161,8 +164,8 @@ def tile_attend_bpagecentred_k_kernel(
         gout_bf = deal_and_round(nc.scalar.copy, gout_raw, "gout_bf")
 
         def load_old(h, tag):
-            part = tile([P, D // P, BANK], F32, f"old{h}", tag=tag)
-            nc.sync.dma_start(out=part[:], in_=old[:, h * BANK : (h + 1) * BANK].rearrange("(j p) u -> p j u", p=P))
+            part = tile([P, 2, U], F32, f"old{h}", tag=tag)
+            nc.sync.dma_start(out=part[:], in_=old[2 * h * P : (2 * h + 2) * P, :].rearrange("(j p) u -> p j u", p=P))
             return part
 
         old_sb = [load_old(0, "query_raw1")]
@@ -213,55 +216,83 @@ def tile_attend_bpagecentred_k_kernel(
             )
 
         db = tile([P, PACK, I], F32, "db")
-        inv, gain, sized, terms, coef = [], [], [], [], []
+        shares, sized = [], []
         for h in range(HALVES):
             rz = tile([P, 2], F32, f"inv{h}")
             nc.vector.reciprocal(out=rz[:], in_=sums[h][:])
-            inv.append(rz)
+            share = tile([P, 2, I], F32, f"share{h}")
+            for rr in range(2):
+                nc.scalar.activation(out=share[:, rr, :], in_=weights[h][:, rr, :], func=ACT.Copy, scale=rz[:, rr : rr + 1])
+            shares.append(share)
+        for h in range(HALVES):
             ps = tile([P, 2, I], F32, f"sized{h}")
-            nc.vector.tensor_tensor(ps[:], weights[h][:], size_row[:].unsqueeze(1).to_broadcast([P, 2, I]), ALU.mult)
+            nc.vector.tensor_tensor(ps[:], shares[h][:], size_row[:].unsqueeze(1).to_broadcast([P, 2, I]), ALU.mult)
             sized.append(ps)
-            k = tile([P, 2], F32, f"gain{h}")
-            nc.vector.tensor_tensor(k[:], inv[h][:], qs_sb[:, 2 * h : 2 * h + 2], ALU.mult)
-            gain.append(k)
+        terms, dots = [], []
         for h in range(HALVES):
             w = tile([P, 2, I], F32, f"terms{h}")
             s = tile([P, 2], F32, f"dots{h}")
             for rr in range(2):
+                r = 2 * h + rr
                 nc.vector.scalar_tensor_tensor(
                     out=w[:, rr, :],
                     in0=value_scores[h][:, rr * I : (rr + 1) * I],
-                    scalar=gain[h][:, rr : rr + 1],
+                    scalar=neg_qs[:, r : r + 1],
                     in1=sized[h][:, rr, :],
                     op0=ALU.mult,
                     op1=ALU.mult,
                     accum_out=s[:, rr : rr + 1],
                 )
-            c = tile([P, 2], F32, f"coef{h}")
-            nc.vector.scalar_tensor_tensor(out=c[:], in0=s[:], scalar=-1.0, in1=inv[h][:], op0=ALU.mult, op1=ALU.mult)
             terms.append(w)
-            coef.append(c)
+            dots.append(s)
         for h in range(HALVES):
             for rr in range(2):
                 nc.vector.scalar_tensor_tensor(
                     out=db[:, 2 * h + rr, :],
-                    in0=weights[h][:, rr, :],
-                    scalar=coef[h][:, rr : rr + 1],
+                    in0=shares[h][:, rr, :],
+                    scalar=dots[h][:, rr : rr + 1],
                     in1=terms[h][:, rr, :],
                     op0=ALU.mult,
-                    op1=ALU.add,
+                    op1=ALU.subtract,
                 )
         qrows_mx = quantize(qrows_bf[:].rearrange("p d t -> p (d t)"), "qrows")
 
-        faded_t = []
-        for c in range(U // P):
-            bank = bank_tile(4 + c % 4, f"old_t{c}")
-            h, cc = divmod(c, BANK // P)
-            for j in range(D // P):
-                nc.tensor.transpose(bank[:, block(j)], old_sb[h][:, j, block(cc)], ident[:])
-            ft = tile([P, D], F32, f"faded_t{c}")
-            nc.scalar.activation(out=ft[:], in_=bank[:], func=ACT.Copy, scale=columns[:, c : c + 1])
-            faded_t.append(ft)
+        blocks = BANK // P
+        faded_t = {}
+
+        def fade_pair(h, banks):
+            for cp in range(U // P // 2):
+                bank = bank_tile(banks[cp % len(banks)], f"old_t{h}_{cp}")
+                for cc in range(2):
+                    for jj in range(2):
+                        nc.tensor.transpose(bank[:, block(2 * cc + jj)], old_sb[h][:, jj, block(2 * cp + cc)], ident[:])
+                for cc in range(2):
+                    c = 2 * cp + cc
+                    ft = tile([P, 2 * P], F32, f"faded_t{h}_{c}")
+                    nc.scalar.activation(
+                        out=ft[:], in_=bank[:, 2 * cc * P : (2 * cc + 2) * P], func=ACT.Copy, scale=columns[:, c : c + 1]
+                    )
+                    faded_t[h, c] = ft
+
+        def turn_back(j, first_bank, keep_open):
+            banks = []
+            for h in range(HALVES):
+                bank = bank_tile(first_bank + h, f"faded{j}_{h}")
+                for cc in range(blocks):
+                    nc.tensor.matmul(
+                        bank[:, block(cc)],
+                        faded_t[j // 2, h * blocks + cc][:, block(j % 2)],
+                        ident[:],
+                        start=(cc == 0 or not keep_open),
+                        stop=not keep_open,
+                        is_transpose=True,
+                    )
+                banks.append(bank)
+            return banks
+
+        fade_pair(0, (4, 5, 6, 7))
+        faded = [turn_back(0, 0, True), turn_back(1, 4, False)]
+        fade_pair(1, (6, 7))
 
         pages = G // HALVES
         shifts = []
@@ -288,7 +319,7 @@ def tile_attend_bpagecentred_k_kernel(
                 ALU.add,
             )
             gs_mx = quantize(gs_bf[:].rearrange("p i r -> p (i r)"), f"gs{h}")
-            bank = bank_tile(h, f"grads{h}")
+            bank = bank_tile(2 + h, f"grads{h}")
             for j in range(D // P):
                 product(bank[:, block(j)], qrows_mx, FP8X4, block(j), gs_mx, FP8X4)
             gk = tile([P, D // P, P], F32, f"gk{h}")
@@ -299,45 +330,32 @@ def tile_attend_bpagecentred_k_kernel(
                 )
             grads.append(gk)
 
-        first_bank = (2, 4, 0, 6)
-        blocks = BANK // P
+        faded.append(turn_back(2, 2, False))
         for j in range(D // P):
             window = scattered[j % 2]
-            on_tensor = j % 2 == 0
-            faded = []
-            for h in range(HALVES):
-                bank = bank_tile(first_bank[j] + h, f"faded{j}_{h}")
-                for cc in range(blocks):
-                    nc.tensor.matmul(
-                        bank[:, block(cc)],
-                        faded_t[h * blocks + cc][:, block(j)],
-                        ident[:],
-                        start=(cc == 0 or not on_tensor),
-                        stop=not on_tensor,
-                        is_transpose=True,
-                    )
-                faded.append(bank)
             for h in range(HALVES):
                 nc.vector.tensor_copy(out=window[:].indirect(places[:, 8 * h : 8 * h + 8]), in_=grads[h][:, j, :])
             for h in range(HALVES):
                 result = tile([P, BANK], F32, f"result{j}_{h}")
                 cols = slice(h * BANK, (h + 1) * BANK)
-                if on_tensor:
-                    bank = bank_tile((6 if j == 0 else 2) + h, f"window_t{j}_{h}")
+                if j == 0:
+                    bank = bank_tile(6 + h, f"window_t{h}")
                     for cc in range(blocks):
                         nc.tensor.transpose(bank[:, block(cc)], window[:, block(h * blocks + cc)], ident[:])
-                    window_t = tile([P, BANK], F32, f"window_t{j}_{h}")
+                    window_t = tile([P, BANK], F32, f"window_t{h}")
                     nc.scalar.copy(out=window_t[:], in_=bank[:])
                     for cc in range(blocks):
                         nc.tensor.matmul(
-                            faded[h][:, block(cc)],
+                            faded[j][h][:, block(cc)],
                             window_t[:, block(cc)],
                             ident[:],
                             start=False,
                             stop=(cc == blocks - 1),
                             is_transpose=True,
                         )
-                    nc.scalar.copy(out=result[:], in_=faded[h][:])
+                    nc.scalar.copy(out=result[:], in_=faded[j][h][:])
                 else:
-                    nc.vector.tensor_tensor(result[:], faded[h][:], window[:, cols], ALU.add)
+                    nc.vector.tensor_tensor(result[:], faded[j][h][:], window[:, cols], ALU.add)
                 nc.sync.dma_start(out=out[block(j), cols], in_=result[:])
+            if j == 0:
+                faded.append(turn_back(3, 6, False))

@@ -54,40 +54,36 @@ def tile_attend_bpagecentred_k_kernel(
             nc.sync.dma_start(out=pool_words[:].bitcast(I32), in_=words[0].bitcast(I32))
             return pool_words
 
-        def load_column_halves(matrix, name):
-            halves = []
-            for h in range(HALVES):
-                raw = tile([P, PACK, Q // HALVES], F32, f"{name}{h}")
-                cols = slice(h * Q // HALVES, (h + 1) * Q // HALVES)
-                nc.sync.dma_start(out=raw[:], in_=matrix[:, cols].rearrange("(p j) c -> p j c", j=PACK))
-                halves.append(raw)
-            return halves
+        def load_column_half(matrix, h, name, tag):
+            raw = tile([P, PACK, Q // HALVES], F32, name, tag=tag)
+            cols = slice(h * Q // HALVES, (h + 1) * Q // HALVES)
+            nc.sync.dma_start(out=raw[:], in_=matrix[:, cols].rearrange("(p j) c -> p j c", j=PACK))
+            return raw
 
         slots = sb.tile([P, I // 16], U16, name="slots")
         nc.sync.dma_start(slots[:], offs)
         places = sb.tile([P, I // 16], U16, name="places")
         nc.sync.dma_start(places[:], offs4)
-        trust_sb = tile([P, PACK], F32, "trust_sb")
-        nc.scalar.dma_start(out=trust_sb[:], in_=trust.rearrange("(p r) o -> p (r o)", r=PACK))
-        qs_sb = tile([P, PACK], F32, "qs_sb")
-        nc.scalar.dma_start(out=qs_sb[:], in_=qs.rearrange("(p r) o -> p (r o)", r=PACK))
-        query_raw = load_column_halves(query, "query_raw")
         key_plane = load_scale_rows(keys_scales, "key_plane")
-        key_pool = load_words(keys_words, "key_pool", "key_pool")
-        gout_raw = load_column_halves(gout, "gout_raw")
+        query_raw = [load_column_half(query, h, f"query_raw{h}", f"stage{h}") for h in range(HALVES)]
+        key_pool = load_words(keys_words, "key_pool", "stage2")
         rows = tile([P, P], F32, "rows")
         nc.gpsimd.memset(rows[:], 0.0)
+        ident = tile([P, P], F32, "ident")
+        make_identity(nc, ident[:])
+        trust_sb = tile([P, PACK], F32, "trust_sb")
+        nc.gpsimd.dma_start(out=trust_sb[:], in_=trust.rearrange("(p r) o -> p (r o)", r=PACK))
+        qs_sb = tile([P, PACK], F32, "qs_sb")
+        nc.gpsimd.dma_start(out=qs_sb[:], in_=qs.rearrange("(p r) o -> p (r o)", r=PACK))
+        warm = tile([P, 1], F32, "warm")
+        nc.scalar.activation(out=warm[:], in_=ident[:, 0:1], func=ACT.Exp)
+        gout_raw = [load_column_half(gout, 0, "gout_raw0", "stage3")]
         nc.scalar.dma_start(out=rows[8:10, :], in_=size.rearrange("o (c p) -> (o c) p", p=P))
         nc.scalar.dma_start(out=rows[0:8, :], in_=fade.rearrange("o (c p) -> (o c) p", p=P))
         val_plane = load_scale_rows(vals_scales, "val_plane")
-        ident = tile([P, P], F32, "ident")
-        make_identity(nc, ident[:])
-
-        warm = tile([P, 1], F32, "warm")
-        nc.scalar.activation(out=warm[:], in_=ident[:, 0:1], func=ACT.Exp)
 
         scattered = []
-        for j in range(2):
+        for j in range(3):
             window = tile([P, U], F32, f"scattered{j}")
             nc.vector.memset(window[:], 0.0)
             scattered.append(window)
@@ -102,8 +98,8 @@ def tile_attend_bpagecentred_k_kernel(
             for h, raw in enumerate(halves):
                 s = slice(h * P // HALVES, (h + 1) * P // HALVES)
                 copy(
-                    out=grouped[:, :, s, :],
-                    in_=raw[:].rearrange("p j (s r) -> p r s j", r=PACK),
+                    out=grouped[:, :, s, :].rearrange("p r s j -> p s j r"),
+                    in_=raw[:].rearrange("p j (s r) -> p s j r", r=PACK),
                 )
             return grouped[:].rearrange("p r s j -> p (r s j)")
 
@@ -139,17 +135,15 @@ def tile_attend_bpagecentred_k_kernel(
             return slice(n * P, (n + 1) * P)
 
         query_bf = deal_and_round(nc.vector.tensor_copy, query_raw, "query_bf")
-        val_pool = load_words(vals_words, "val_pool", "query_raw0")
+        gout_raw.append(load_column_half(gout, 1, "gout_raw1", "stage0"))
+        val_pool = load_words(vals_words, "val_pool", "stage1")
         key_scales = gather(key_plane, U8, "key_scales")
         query_mx = quantize(query_bf, "query")
         key_words = gather(key_pool, U16, "key_words")
         scores = rows_times_listed(query_mx, (key_words, key_scales), 0, "scores")
 
         neg_trust = tile([P, PACK], F32, "neg_trust")
-        nc.vector.tensor_scalar(neg_trust[:], trust_sb[:], -1.0 / PAGE, None, ALU.mult)
-
-        neg_qs = tile([P, PACK], F32, "neg_qs")
-        nc.vector.tensor_scalar(neg_qs[:], qs_sb[:], -1.0, None, ALU.mult)
+        nc.scalar.activation(out=neg_trust[:], in_=trust_sb[:], func=ACT.Copy, scale=-1.0 / PAGE)
 
         turned = bank_tile(4, "turned")
         nc.tensor.transpose(turned[:, 0:P], rows[:], ident[:])
@@ -168,10 +162,10 @@ def tile_attend_bpagecentred_k_kernel(
             nc.sync.dma_start(out=part[:], in_=old[2 * h * P : (2 * h + 2) * P, :].rearrange("(j p) u -> p j u", p=P))
             return part
 
-        old_sb = [load_old(0, "query_raw1")]
-        qrows_raw = tile([P, PACK, D], F32, "qrows_raw", tag="gout_raw0")
+        old_sb = [load_old(0, "stage2")]
+        qrows_raw = tile([P, PACK, D], F32, "qrows_raw", tag="stage3")
         nc.sync.dma_start(out=qrows_raw[:], in_=qrows.rearrange("(p t) d -> p t d", t=PACK))
-        old_sb.append(load_old(1, "gout_raw1"))
+        old_sb.append(load_old(1, "stage0"))
 
         val_scales = gather(val_plane, U8, "val_scales")
         val_words = gather(val_pool, U16, "val_words")
@@ -216,44 +210,43 @@ def tile_attend_bpagecentred_k_kernel(
             )
 
         db = tile([P, PACK, I], F32, "db")
-        shares, sized = [], []
+        inv, gain, sized, terms, coef = [], [], [], [], []
         for h in range(HALVES):
             rz = tile([P, 2], F32, f"inv{h}")
             nc.vector.reciprocal(out=rz[:], in_=sums[h][:])
-            share = tile([P, 2, I], F32, f"share{h}")
-            for rr in range(2):
-                nc.scalar.activation(out=share[:, rr, :], in_=weights[h][:, rr, :], func=ACT.Copy, scale=rz[:, rr : rr + 1])
-            shares.append(share)
-        for h in range(HALVES):
+            inv.append(rz)
             ps = tile([P, 2, I], F32, f"sized{h}")
-            nc.vector.tensor_tensor(ps[:], shares[h][:], size_row[:].unsqueeze(1).to_broadcast([P, 2, I]), ALU.mult)
+            nc.vector.tensor_tensor(ps[:], weights[h][:], size_row[:].unsqueeze(1).to_broadcast([P, 2, I]), ALU.mult)
             sized.append(ps)
-        terms, dots = [], []
+            k = tile([P, 2], F32, f"gain{h}")
+            nc.vector.tensor_tensor(k[:], inv[h][:], qs_sb[:, 2 * h : 2 * h + 2], ALU.mult)
+            gain.append(k)
         for h in range(HALVES):
             w = tile([P, 2, I], F32, f"terms{h}")
             s = tile([P, 2], F32, f"dots{h}")
             for rr in range(2):
-                r = 2 * h + rr
                 nc.vector.scalar_tensor_tensor(
                     out=w[:, rr, :],
                     in0=value_scores[h][:, rr * I : (rr + 1) * I],
-                    scalar=neg_qs[:, r : r + 1],
+                    scalar=gain[h][:, rr : rr + 1],
                     in1=sized[h][:, rr, :],
                     op0=ALU.mult,
                     op1=ALU.mult,
                     accum_out=s[:, rr : rr + 1],
                 )
+            c = tile([P, 2], F32, f"coef{h}")
+            nc.vector.scalar_tensor_tensor(out=c[:], in0=s[:], scalar=-1.0, in1=inv[h][:], op0=ALU.mult, op1=ALU.mult)
             terms.append(w)
-            dots.append(s)
+            coef.append(c)
         for h in range(HALVES):
             for rr in range(2):
                 nc.vector.scalar_tensor_tensor(
                     out=db[:, 2 * h + rr, :],
-                    in0=shares[h][:, rr, :],
-                    scalar=dots[h][:, rr : rr + 1],
+                    in0=weights[h][:, rr, :],
+                    scalar=coef[h][:, rr : rr + 1],
                     in1=terms[h][:, rr, :],
                     op0=ALU.mult,
-                    op1=ALU.subtract,
+                    op1=ALU.add,
                 )
         qrows_mx = quantize(qrows_bf[:].rearrange("p d t -> p (d t)"), "qrows")
 
@@ -291,7 +284,12 @@ def tile_attend_bpagecentred_k_kernel(
             return banks
 
         fade_pair(0, (4, 5, 6, 7))
-        faded = [turn_back(0, 0, True), turn_back(1, 4, False)]
+        def to_sbuf(bank, name):
+            held = tile([P, BANK], F32, name)
+            nc.scalar.copy(out=held[:], in_=bank[:])
+            return held[:]
+
+        faded = [turn_back(0, 0, True), [to_sbuf(bank, f"faded_sb1_{h}") for h, bank in enumerate(turn_back(1, 4, False))]]
         fade_pair(1, (6, 7))
 
         pages = G // HALVES
@@ -309,7 +307,7 @@ def tile_attend_bpagecentred_k_kernel(
                 ALU.mult,
             )
             shifts.append(shift)
-        grads = []
+        grad_banks = [bank_tile(2 + pair, f"grads{pair}") for pair in range(2)]
         for h in range(HALVES):
             gs_bf = tile([P, P, PACK], BF16, f"gs_bf{h}")
             nc.vector.tensor_tensor(
@@ -319,22 +317,20 @@ def tile_attend_bpagecentred_k_kernel(
                 ALU.add,
             )
             gs_mx = quantize(gs_bf[:].rearrange("p i r -> p (i r)"), f"gs{h}")
-            bank = bank_tile(2 + h, f"grads{h}")
             for j in range(D // P):
-                product(bank[:, block(j)], qrows_mx, FP8X4, block(j), gs_mx, FP8X4)
-            gk = tile([P, D // P, P], F32, f"gk{h}")
-            for pair in range(2):
-                nc.scalar.copy(
-                    out=gk[:, 2 * pair : 2 * pair + 2, :].rearrange("p j i -> p (j i)"),
-                    in_=bank[:, 2 * pair * P : (2 * pair + 2) * P],
-                )
+                product(grad_banks[j // 2][:, block(2 * (j % 2) + h)], qrows_mx, FP8X4, block(j), gs_mx, FP8X4)
+        grads = []
+        for j in range(D // P):
+            gk = tile([P, I], F32, f"gk{j}")
+            nc.scalar.copy(out=gk[:], in_=grad_banks[j // 2][:, (j % 2) * I : (j % 2 + 1) * I])
             grads.append(gk)
 
-        faded.append(turn_back(2, 2, False))
+        third = turn_back(2, 4, False)
+        faded.append([to_sbuf(third[0], "faded_sb2"), third[1][:]])
+        faded.append([bank[:] for bank in turn_back(3, 2, False)])
         for j in range(D // P):
-            window = scattered[j % 2]
-            for h in range(HALVES):
-                nc.vector.tensor_copy(out=window[:].indirect(places[:, 8 * h : 8 * h + 8]), in_=grads[h][:, j, :])
+            window = scattered[j % 3]
+            nc.vector.tensor_copy(out=window[:].indirect(places[:]), in_=grads[j][:])
             for h in range(HALVES):
                 result = tile([P, BANK], F32, f"result{j}_{h}")
                 cols = slice(h * BANK, (h + 1) * BANK)
@@ -342,8 +338,7 @@ def tile_attend_bpagecentred_k_kernel(
                     bank = bank_tile(6 + h, f"window_t{h}")
                     for cc in range(blocks):
                         nc.tensor.transpose(bank[:, block(cc)], window[:, block(h * blocks + cc)], ident[:])
-                    window_t = tile([P, BANK], F32, f"window_t{h}")
-                    nc.scalar.copy(out=window_t[:], in_=bank[:])
+                    window_t = to_sbuf(bank, f"window_t{h}")
                     for cc in range(blocks):
                         nc.tensor.matmul(
                             faded[j][h][:, block(cc)],
@@ -355,7 +350,6 @@ def tile_attend_bpagecentred_k_kernel(
                         )
                     nc.scalar.copy(out=result[:], in_=faded[j][h][:])
                 else:
-                    nc.vector.tensor_tensor(result[:], faded[j][h][:], window[:, cols], ALU.add)
+                    engine = nc.gpsimd if 2 * j + h < 5 else nc.vector
+                    engine.tensor_tensor(result[:], faded[j][h], window[:, cols], ALU.add)
                 nc.sync.dma_start(out=out[block(j), cols], in_=result[:])
-            if j == 0:
-                faded.append(turn_back(3, 6, False))

from contextlib import ExitStack

import concourse.mybir as mybir
from concourse.masks import make_identity

D, E, T, I, Q, G, U = 512, 512, 2048, 256, 512, 16, 1024
FLOPS = 2 * Q * I * (D + E + D)

F32 = mybir.dt.float32
BF16 = mybir.dt.bfloat16
I32 = mybir.dt.int32
U32 = mybir.dt.uint32
U16 = mybir.dt.uint16
U8 = mybir.dt.uint8
FP8X4 = mybir.dt.float8_e4m3fn_x4
FP4X4 = mybir.dt.float4_e2m1fn_x4
ALU = mybir.AluOpType
ACT = mybir.ActivationFunctionType
AXIS_X = mybir.AxisListType.X

P = 128
PACK = 4
PAGE = I // G
BANK = 512
HALVES = 2


def tile_attend_bpagecentred_k_kernel(
    tc, query, keys_words, keys_scales, trust, gout, vals_words, vals_scales, size, qs, qrows, old, fade, offs, offs4, out
):
    nc = tc.nc
    with ExitStack() as ctx:
        sb = ctx.enter_context(tc.tile_pool(name="sb", bufs=1))
        psum = ctx.enter_context(tc.psum_pool(name="psum", bufs=1))

        def bank_tile(number, name):
            return psum.tile([P, BANK], F32, name=name, tag=f"bank{number}")

        def tile(shape, dtype, name, tag=None):
            return sb.tile(shape, dtype, name=name, tag=tag or name, align_bytes=64)

        def load_scale_rows(scales, name):
            plane = tile([P, T], U8, name)
            nc.vector.memset(plane[:].bitcast(I32), 0)
            for quad in range(4):
                nc.scalar.dma_start(
                    out=plane[32 * quad : 32 * quad + 4, :].bitcast(I32),
                    in_=scales[0, 4 * quad : 4 * quad + 4, :].bitcast(I32),
                )
            return plane

        def load_words(words, name, tag):
            pool_words = tile([P, T], U16, name, tag=tag)
            nc.sync.dma_start(out=pool_words[:].bitcast(I32), in_=words[0].bitcast(I32))
            return pool_words

        def load_column_half(matrix, h, name, tag):
            raw = tile([P, PACK, Q // HALVES], F32, name, tag=tag)
            cols = slice(h * Q // HALVES, (h + 1) * Q // HALVES)
            nc.sync.dma_start(out=raw[:], in_=matrix[:, cols].rearrange("(p j) c -> p j c", j=PACK))
            return raw

        slots = sb.tile([P, I // 16], U16, name="slots")
        nc.sync.dma_start(slots[:], offs)
        places = sb.tile([P, I // 16], U16, name="places")
        nc.sync.dma_start(places[:], offs4)
        key_plane = load_scale_rows(keys_scales, "key_plane")
        query_raw = [load_column_half(query, h, f"query_raw{h}", f"stage{h}") for h in range(HALVES)]
        key_pool = load_words(keys_words, "key_pool", "stage2")
        rows = tile([P, P], F32, "rows")
        nc.gpsimd.memset(rows[:], 0.0)
        ident = tile([P, P], F32, "ident")
        make_identity(nc, ident[:])
        trust_sb = tile([P, PACK], F32, "trust_sb")
        nc.gpsimd.dma_start(out=trust_sb[:], in_=trust.rearrange("(p r) o -> p (r o)", r=PACK))
        qs_sb = tile([P, PACK], F32, "qs_sb")
        nc.gpsimd.dma_start(out=qs_sb[:], in_=qs.rearrange("(p r) o -> p (r o)", r=PACK))
        warm = tile([P, 1], F32, "warm")
        nc.scalar.activation(out=warm[:], in_=ident[:, 0:1], func=ACT.Exp)
        gout_raw = [load_column_half(gout, 0, "gout_raw0", "stage3")]
        nc.scalar.dma_start(out=rows[8:10, :], in_=size.rearrange("o (c p) -> (o c) p", p=P))
        nc.scalar.dma_start(out=rows[0:8, :], in_=fade.rearrange("o (c p) -> (o c) p", p=P))
        val_plane = load_scale_rows(vals_scales, "val_plane")

        scattered = []
        for j in range(3):
            window = tile([P, U], F32, f"scattered{j}")
            nc.vector.memset(window[:], 0.0)
            scattered.append(window)

        def gather(pool_tile, dtype, name):
            picked = tile([P, I], dtype, name)
            nc.vector.tensor_copy(out=picked[:], in_=pool_tile[:].indirect(slots[:]))
            return picked

        def deal_and_round(copy, halves, name):
            grouped = tile([P, PACK, P, PACK], BF16, name)
            for h, raw in enumerate(halves):
                s = slice(h * P // HALVES, (h + 1) * P // HALVES)
                copy(
                    out=grouped[:, :, s, :].rearrange("p r s j -> p s j r"),
                    in_=raw[:].rearrange("p j (s r) -> p s j r", r=PACK),
                )
            return grouped[:].rearrange("p r s j -> p (r s j)")

        def quantize(values, name):
            width = values.shape[1] // PACK
            codes = tile([P, width], U32, name + "_codes")
            scales = tile([P, width], U8, name + "_scales")
            nc.vector.quantize_mx(out=codes[:].bitcast(FP8X4), scales=scales[:], in_=values)
            return codes, scales

        def product(out_cols, lhs, lhs_dtype, lhs_cols, rhs, rhs_dtype):
            nc.tensor.matmul_mx(
                out=out_cols,
                lhsT=lhs[0][:, lhs_cols].bitcast(lhs_dtype),
                lhsT_scale=lhs[1][:, lhs_cols],
                rhs=rhs[0][:].bitcast(rhs_dtype),
                rhs_scale=rhs[1][:],
                start=True,
                stop=True,
            )

        def rows_times_listed(row_operand, listed, first_bank, name):
            banks = []
            for h in range(HALVES):
                bank = bank_tile(first_bank + h, f"{name}{h}")
                for rr in range(2):
                    r = 2 * h + rr
                    product(bank[:, rr * I : (rr + 1) * I], row_operand, FP8X4, slice(r * P, (r + 1) * P), listed, FP4X4)
                banks.append(bank)
            return banks

        def block(n):
            return slice(n * P, (n + 1) * P)

        query_bf = deal_and_round(nc.vector.tensor_copy, query_raw, "query_bf")
        gout_raw.append(load_column_half(gout, 1, "gout_raw1", "stage0"))
        val_pool = load_words(vals_words, "val_pool", "stage1")
        key_scales = gather(key_plane, U8, "key_scales")
        query_mx = quantize(query_bf, "query")
        key_words = gather(key_pool, U16, "key_words")
        scores = rows_times_listed(query_mx, (key_words, key_scales), 0, "scores")

        neg_trust = tile([P, PACK], F32, "neg_trust")
        nc.scalar.activation(out=neg_trust[:], in_=trust_sb[:], func=ACT.Copy, scale=-1.0 / PAGE)

        turned = bank_tile(4, "turned")
        nc.tensor.transpose(turned[:, 0:P], rows[:], ident[:])
        columns = tile([P, 16], F32, "columns")
        nc.scalar.copy(out=columns[:], in_=turned[:, 0:16])
        spread = bank_tile(5, "spread")
        for c in range(I // P):
            nc.tensor.transpose(spread[:, block(c)], columns[:, 8 + c : 9 + c].to_broadcast([P, P]), ident[:])
        size_row = tile([P, I], F32, "size_row")
        nc.scalar.copy(out=size_row[:], in_=spread[:, 0:I])

        gout_bf = deal_and_round(nc.scalar.copy, gout_raw, "gout_bf")

        def load_old(h, tag):
            part = tile([P, 2, U], F32, f"old{h}", tag=tag)
            nc.sync.dma_start(out=part[:], in_=old[2 * h * P : (2 * h + 2) * P, :].rearrange("(j p) u -> p j u", p=P))
            return part

        old_sb = [load_old(0, "stage2")]
        qrows_raw = tile([P, PACK, D], F32, "qrows_raw", tag="stage3")
        nc.sync.dma_start(out=qrows_raw[:], in_=qrows.rearrange("(p t) d -> p t d", t=PACK))
        old_sb.append(load_old(1, "stage0"))

        val_scales = gather(val_plane, U8, "val_scales")
        val_words = gather(val_pool, U16, "val_words")
        gout_mx = quantize(gout_bf, "gout")
        value_scores = rows_times_listed(gout_mx, (val_words, val_scales), 2, "value_scores")

        centred, weights, sums = [], [], []
        for h in range(HALVES):
            page_sum = tile([P, 2 * G], F32, f"page_sum{h}")
            nc.vector.tensor_reduce(
                out=page_sum[:], in_=scores[h][:].rearrange("p (g j) -> p g j", j=PAGE), axis=AXIS_X, op=ALU.add
            )
            b = tile([P, 2, I], F32, f"centred{h}")
            for rr in range(2):
                r = 2 * h + rr
                nc.vector.scalar_tensor_tensor(
                    out=b[:, rr, :].rearrange("p (g j) -> p g j", j=PAGE),
                    in0=page_sum[:, rr * G : (rr + 1) * G].unsqueeze(2).to_broadcast([P, G, PAGE]),
                    scalar=neg_trust[:, r : r + 1],
                    in1=scores[h][:, rr * I : (rr + 1) * I].rearrange("p (g j) -> p g j", j=PAGE),
                    op0=ALU.mult,
                    op1=ALU.add,
                )
            centred.append(b)
        for h in range(HALVES):
            m = tile([P, 2], F32, f"neg_max{h}")
            nc.vector.tensor_reduce(out=m[:], in_=centred[h][:], axis=AXIS_X, op=ALU.max, negate=True)
            p = tile([P, 2, I], F32, f"weights{h}")
            z = tile([P, 2], F32, f"sums{h}")
            for rr in range(2):
                nc.scalar.activation(
                    out=p[:, rr, :], in_=centred[h][:, rr, :], func=ACT.Exp, bias=m[:, rr : rr + 1], accum_out=z[:, rr : rr + 1]
                )
            weights.append(p)
            sums.append(z)

        qrows_bf = tile([P, D, PACK], BF16, "qrows_bf")
        for j in range(D // P):
            nc.scalar.copy(
                out=qrows_bf[:, block(j), :].rearrange("p (c i) t -> p c t i", i=4),
                in_=qrows_raw[:, :, block(j)].rearrange("p t (c i) -> p c t i", i=4),
            )

        db = tile([P, PACK, I], F32, "db")
        inv, gain, sized, terms, coef = [], [], [], [], []
        for h in range(HALVES):
            rz = tile([P, 2], F32, f"inv{h}")
            nc.vector.reciprocal(out=rz[:], in_=sums[h][:])
            inv.append(rz)
            ps = tile([P, 2, I], F32, f"sized{h}")
            nc.vector.tensor_tensor(ps[:], weights[h][:], size_row[:].unsqueeze(1).to_broadcast([P, 2, I]), ALU.mult)
            sized.append(ps)
            k = tile([P, 2], F32, f"gain{h}")
            nc.vector.tensor_tensor(k[:], inv[h][:], qs_sb[:, 2 * h : 2 * h + 2], ALU.mult)
            gain.append(k)
        for h in range(HALVES):
            w = tile([P, 2, I], F32, f"terms{h}")
            s = tile([P, 2], F32, f"dots{h}")
            for rr in range(2):
                nc.vector.scalar_tensor_tensor(
                    out=w[:, rr, :],
                    in0=value_scores[h][:, rr * I : (rr + 1) * I],
                    scalar=gain[h][:, rr : rr + 1],
                    in1=sized[h][:, rr, :],
                    op0=ALU.mult,
                    op1=ALU.mult,
                    accum_out=s[:, rr : rr + 1],
                )
            c = tile([P, 2], F32, f"coef{h}")
            nc.vector.scalar_tensor_tensor(out=c[:], in0=s[:], scalar=-1.0, in1=inv[h][:], op0=ALU.mult, op1=ALU.mult)
            terms.append(w)
            coef.append(c)
        for h in range(HALVES):
            for rr in range(2):
                nc.vector.scalar_tensor_tensor(
                    out=db[:, 2 * h + rr, :],
                    in0=weights[h][:, rr, :],
                    scalar=coef[h][:, rr : rr + 1],
                    in1=terms[h][:, rr, :],
                    op0=ALU.mult,
                    op1=ALU.add,
                )
        qrows_mx = quantize(qrows_bf[:].rearrange("p d t -> p (d t)"), "qrows")

        blocks = BANK // P
        faded_t = {}

        def fade_pair(h, banks):
            for cp in range(U // P // 2):
                bank = bank_tile(banks[cp % len(banks)], f"old_t{h}_{cp}")
                for cc in range(2):
                    for jj in range(2):
                        nc.tensor.transpose(bank[:, block(2 * cc + jj)], old_sb[h][:, jj, block(2 * cp + cc)], ident[:])
                for cc in range(2):
                    c = 2 * cp + cc
                    ft = tile([P, 2 * P], F32, f"faded_t{h}_{c}")
                    nc.scalar.activation(
                        out=ft[:], in_=bank[:, 2 * cc * P : (2 * cc + 2) * P], func=ACT.Copy, scale=columns[:, c : c + 1]
                    )
                    faded_t[h, c] = ft

        def turn_back(j, first_bank, keep_open):
            banks = []
            for h in range(HALVES):
                bank = bank_tile(first_bank + h, f"faded{j}_{h}")
                for cc in range(blocks):
                    nc.tensor.matmul(
                        bank[:, block(cc)],
                        faded_t[j // 2, h * blocks + cc][:, block(j % 2)],
                        ident[:],
                        start=(cc == 0 or not keep_open),
                        stop=not keep_open,
                        is_transpose=True,
                    )
                banks.append(bank)
            return banks

        fade_pair(0, (4, 5, 6, 7))
        def to_sbuf(bank, name):
            held = tile([P, BANK], F32, name)
            nc.scalar.copy(out=held[:], in_=bank[:])
            return held[:]

        faded = [turn_back(0, 0, True), [to_sbuf(bank, f"faded_sb1_{h}") for h, bank in enumerate(turn_back(1, 4, False))]]
        fade_pair(1, (6, 7))

        pages = G // HALVES
        shifts = []
        for h in range(HALVES):
            page_db = tile([P, PACK, pages], F32, f"page_db{h}")
            nc.vector.tensor_reduce(
                out=page_db[:], in_=db[:, :, block(h)].rearrange("p r (g j) -> p r g j", j=PAGE), axis=AXIS_X, op=ALU.add
            )
            shift = tile([P, pages, PACK], F32, f"shift{h}")
            nc.vector.tensor_tensor(
                shift[:].rearrange("p g r -> p r g"),
                page_db[:],
                neg_trust[:].unsqueeze(2).to_broadcast([P, PACK, pages]),
                ALU.mult,
            )
            shifts.append(shift)
        grad_banks = [bank_tile(2 + pair, f"grads{pair}") for pair in range(2)]
        for h in range(HALVES):
            gs_bf = tile([P, P, PACK], BF16, f"gs_bf{h}")
            nc.vector.tensor_tensor(
                gs_bf[:].rearrange("p (g j) r -> p g j r", j=PAGE),
                db[:, :, block(h)].rearrange("p r (g j) -> p g j r", j=PAGE),
                shifts[h][:].unsqueeze(2).to_broadcast([P, pages, PAGE, PACK]),
                ALU.add,
            )
            gs_mx = quantize(gs_bf[:].rearrange("p i r -> p (i r)"), f"gs{h}")
            for j in range(D // P):
                product(grad_banks[j // 2][:, block(2 * (j % 2) + h)], qrows_mx, FP8X4, block(j), gs_mx, FP8X4)
        grads = []
        for j in range(D // P):
            gk = tile([P, I], F32, f"gk{j}")
            nc.scalar.copy(out=gk[:], in_=grad_banks[j // 2][:, (j % 2) * I : (j % 2 + 1) * I])
            grads.append(gk)

        third = turn_back(2, 4, False)
        faded.append([to_sbuf(third[0], "faded_sb2"), third[1][:]])
        faded.append([bank[:] for bank in turn_back(3, 2, False)])
        for j in range(D // P):
            window = scattered[j % 3]
            nc.vector.tensor_copy(out=window[:].indirect(places[:]), in_=grads[j][:])
            for h in range(HALVES):
                result = tile([P, BANK], F32, f"result{j}_{h}")
                cols = slice(h * BANK, (h + 1) * BANK)
                if j == 0:
                    bank = bank_tile(6 + h, f"window_t{h}")
                    for cc in range(blocks):
                        nc.tensor.transpose(bank[:, block(cc)], window[:, block(h * blocks + cc)], ident[:])
                    window_t = to_sbuf(bank, f"window_t{h}")
                    for cc in range(blocks):
                        nc.tensor.matmul(
                            faded[j][h][:, block(cc)],
                            window_t[:, block(cc)],
                            ident[:],
                            start=False,
                            stop=(cc == blocks - 1),
                            is_transpose=True,
                        )
                    nc.scalar.copy(out=result[:], in_=faded[j][h][:])
                else:
                    engine = nc.gpsimd if 2 * j + h < 5 else nc.vector
                    engine.tensor_tensor(result[:], faded[j][h], window[:, cols], ALU.add)
                nc.sync.dma_start(out=out[block(j), cols], in_=result[:])
